import numpy as np
import ml_dtypes


def mxq(x, axis, fmt="e4m3"):
    dtype, down = {"e4m3": (ml_dtypes.float8_e4m3fn, 7), "e5m2": (ml_dtypes.float8_e5m2, 14)}[fmt]
    v = np.moveaxis(np.asarray(x, np.float32).astype(ml_dtypes.bfloat16).astype(np.float64), axis, -1)
    blocks = v.reshape(v.shape[:-1] + (-1, 32))
    amax = np.abs(blocks).max(-1, keepdims=True)
    byte = np.maximum(np.where(amax > 0, np.frexp(amax)[1] - 1 + 127, 0) - down, 1)
    scale = np.exp2(byte - 127.0)
    codes = (blocks / scale).astype(np.float32).astype(dtype).astype(np.float64)
    return np.moveaxis((codes * scale).reshape(v.shape), -1, axis)


WIDE = False


def mx_kscale(k):
    if not WIDE:
        return np.ones(k)
    levels = np.array([10, -10, 5, -5, 0])
    if k % 512:
        return np.exp2(np.random.permutation(np.resize(levels, k // 32))).repeat(32)
    a = np.empty((k // 512, 16))
    for p in range(k // 512):
        a[p, :8] = np.random.permutation(np.resize(levels, 8))
        for g in range(8):
            far = levels[np.abs(levels - a[p, g]) >= 10]
            a[p, g + 8] = far[np.random.randint(len(far))]
    return np.exp2(a.ravel()).repeat(32)


def f64(x):
    return np.asarray(x).astype(np.float64)


def striped(idx):
    return np.tile(idx.reshape(-1, 16).T, (8, 1)).astype(np.uint16)


def unstriped(offs):
    return offs[:16].T.reshape(-1).astype(np.int64)


def striped8(idx):
    return np.concatenate([x.reshape(-1, 16).T for x in idx]).astype(np.uint16)


def runs(offs, k):
    lists = np.stack([offs[16 * r : 16 * r + 16].T.reshape(-1) for r in range(8)]).astype(np.int64)
    return lists[np.arange(k) % 512 // 64]


def pack_weight(w):
    k, n = w.shape
    w = f64(np.asarray(w, np.float32).astype(ml_dtypes.bfloat16)).reshape(k // 32, 32, n)
    amax = np.abs(w).max(1)
    byte = np.clip(np.where(amax > 0, np.frexp(amax)[1] - 1 + 127 - 7, 1), 1, 254)
    scaled = (w * np.exp2(127.0 - byte)[:, None, :]).reshape(k, n).astype(np.float32)
    words = np.ascontiguousarray(scaled.reshape(k // 512, 128, 4, n).transpose(0, 1, 3, 2)).astype(ml_dtypes.float8_e4m3fn).view(np.uint8)
    return words, np.ascontiguousarray(byte.astype(np.uint8).reshape(k // 512, 16, n))


def unpack_weight(words, scales):
    g, p, n, _ = words.shape
    vals = np.ascontiguousarray(words).view(ml_dtypes.float8_e4m3fn).astype(np.float64) * np.repeat(np.exp2(scales.astype(np.float64) - 127.0), 8, axis=1)[..., None]
    return vals.transpose(0, 1, 3, 2).reshape(g * 512, n)


E2M1 = np.array([0.0, 0.5, 1.0, 1.5, 2.0, 3.0, 4.0, 6.0, -0.0, -0.5, -1.0, -1.5, -2.0, -3.0, -4.0, -6.0])


def pack_fp4(w):
    k, n = w.shape
    w = f64(np.asarray(w, np.float32).astype(ml_dtypes.bfloat16)).reshape(k // 32, 32, n)
    amax = np.abs(w).max(1)
    mant, ex = np.frexp(amax / 6.0)
    byte = np.clip(np.where(amax > 0, np.where(mant > 0.5, ex, ex - 1) + 127, 1), 1, 254)
    scaled = (w * np.exp2(127.0 - byte)[:, None, :]).reshape(k, n).astype(np.float32)
    c = np.ascontiguousarray(scaled.reshape(k // 512, 128, 4, n).transpose(0, 1, 3, 2)).astype(ml_dtypes.float4_e2m1fn).view(np.uint8) & 0xF
    words = (c[..., 0::2] | (c[..., 1::2] << 4)).reshape(k // 512, 128, 2 * n)
    return np.ascontiguousarray(words), np.ascontiguousarray(byte.astype(np.uint8).reshape(k // 512, 16, n))


def unpack_fp4(words, scales):
    g, _, n = scales.shape
    words = np.ascontiguousarray(words).reshape(g, 128, n, 2)
    nib = np.empty((g, 128, n, 4), np.uint8)
    nib[..., 0::2] = words & 0xF
    nib[..., 1::2] = words >> 4
    vals = E2M1[nib] * np.repeat(np.exp2(scales.astype(np.float64) - 127.0), 8, axis=1)[..., None]
    return vals.transpose(0, 1, 3, 2).reshape(g * 512, n)


def relu(v):
    return np.maximum(v, 0.0)

def planes(y):
    n, m = y.shape
    v = y.astype(np.float32).astype(ml_dtypes.bfloat16).astype(np.float64).reshape(n // 32, 32, m)
    top = np.abs(v).max(1)
    byte = np.clip(np.where(top > 0, np.frexp(top)[1] - 1 + 127 - 7, 1), 1, 254)
    codes = (v * np.exp2(127.0 - byte)[:, None, :]).reshape(n, m).astype(np.float32).astype(ml_dtypes.float8_e4m3fn).view(np.uint8)
    words = codes.reshape(n // 512, 128, 4, m).transpose(0, 1, 3, 2)
    return np.ascontiguousarray(words), np.ascontiguousarray(byte.astype(np.uint8).reshape(n // 512, 16, m))


K, T, S, N, G, H = 512, 2048, 512, 512, 2048, 512


def setup_inputs():
    n = np.random.standard_normal
    s = mx_kscale(K)[:, None]
    u = mx_kscale(S)
    packed_xT = pack_weight(n((K, T)) * s)
    packed_dT = pack_weight(n((K, G)) / s)
    packed_w1 = pack_fp4(n((H, N)) / np.sqrt(H) / u[:, None])
    return {
        "x_words": packed_xT[0],
        "x_scales": packed_xT[1],
        "d_words": packed_dT[0],
        "d_scales": packed_dT[1],
        "gn": (np.random.uniform(0.5, 1.5, (H, 1)) * u[:, None]).astype(np.float32),
        "w1_words": packed_w1[0],
        "w1_scales": packed_w1[1],
        "offs": striped(np.random.permutation(T)[:S]),
        "kidx": striped8(np.random.randint(0, G, (8, H))),
        "n1": striped8(np.stack([np.random.permutation(S) for _ in range(8)])),
        "n2": striped8(np.stack([np.random.permutation(S) for _ in range(8)])),
        "n3": striped8(np.stack([np.random.permutation(S) for _ in range(8)])),
        "n4": striped8(np.stack([np.random.permutation(S) for _ in range(8)])),
    }


def reference(x_words, x_scales, d_words, d_scales, gn, w1_words, w1_scales, offs, kidx, n1, n2, n3, n4):
    d_kidx = unpack_weight(d_words, d_scales)[np.arange(K)[:, None], runs(kidx, K)]
    xq = unpack_weight(x_words, x_scales)[:, unstriped(offs)]
    s = 0.0625 * (d_kidx.T @ xq)
    z = f64(gn) * ((s[np.arange(H)[:, None], runs(n1, H)]) * (s[np.arange(H)[:, None], runs(n2, H)]))
    h = unpack_fp4(w1_words, w1_scales).T @ mxq(z, 0, "e4m3")
    out_0 = relu(h - (h[np.arange(N)[:, None], runs(n3, N)])) + 0.5 * (relu(h[np.arange(N)[:, None], runs(n4, N)] - h))
    return (out_0,) + planes(out_0)

@@ -1,0 +1,219 @@
+from contextlib import ExitStack
+
+import concourse.mybir as mybir
+
+K, T, S, N, G, H = 512, 2048, 512, 512, 2048, 512
+FLOPS = 2 * K * H * S + 2 * H * N * S
+
+F32 = mybir.dt.float32
+BF16 = mybir.dt.bfloat16
+I32 = mybir.dt.int32
+U32 = mybir.dt.uint32
+U16 = mybir.dt.uint16
+U8 = mybir.dt.uint8
+FP8X4 = mybir.dt.float8_e4m3fn_x4
+FP4X4 = mybir.dt.float4_e2m1fn_x4
+ALU = mybir.AluOpType
+ACT = mybir.ActivationFunctionType
+
+P = 128
+PACK = 4
+CHUNKS = ((0, 256), (256, 128), (384, 128))
+
+
+def entries(lst, start, width):
+    return lst[:, start // 16 : (start + width) // 16]
+
+
+def tile_picked_keyprodhinge_none_po_kernel(
+    tc, x_words, x_scales, d_words, d_scales, gn, w1_words, w1_scales, offs, kidx, n1, n2, n3, n4, out_0, out_1, out_2
+):
+    nc = tc.nc
+    with ExitStack() as ctx:
+        lists = ctx.enter_context(tc.tile_pool(name="lists", bufs=1))
+        keep = ctx.enter_context(tc.tile_pool(name="keep", bufs=1))
+        psum = ctx.enter_context(tc.psum_pool(name="psum", bufs=1))
+
+        def sb(name, shape, dtype, tag=None):
+            return keep.tile(shape, dtype, name=name, tag=tag or name, align_bytes=64)
+
+        lk = lists.tile([P, H // 16], U16, name="lk")
+        lo = lists.tile([P, S // 16], U16, name="lo")
+        l1 = lists.tile([P, S // 16], U16, name="l1")
+        l2 = lists.tile([P, S // 16], U16, name="l2")
+        l3 = lists.tile([P, S // 16], U16, name="l3")
+        l4 = lists.tile([P, S // 16], U16, name="l4")
+
+        ds = sb("ds", [P, G], U8)
+        xs = sb("xs", [P, T], U8)
+        dw = sb("dw", [P, G], I32)
+        xw = sb("xw", [P, T], I32)
+        ww = sb("ww", [P, 2 * N], U8)
+        gain = sb("gain", [P, PACK], F32)
+        gsc = sb("gsc", [P, PACK], F32)
+
+        nc.vector.memset(ds[:].bitcast(I32), 0)
+        nc.vector.memset(xs[:].bitcast(I32), 0)
+
+        nc.sync.dma_start(lk[:], kidx)
+        d_rows = d_scales[0].rearrange("(g e) c -> e g c", e=2)
+        for e in range(2):
+            nc.scalar.dma_start(ds[e:P:16, :].bitcast(I32), d_rows[e].bitcast(I32))
+        x_rows = x_scales[0].rearrange("(q r) c -> r q c", r=4)
+        for r in range(4):
+            nc.scalar.dma_start(xs[4 + r : P : 32, :].bitcast(I32), x_rows[r].bitcast(I32))
+        nc.sync.dma_start(dw[:], d_words[0].rearrange("p c r -> p (c r)").bitcast(I32))
+        nc.sync.dma_start(lo[:], offs)
+        nc.sync.dma_start(gain[:], gn.rearrange("(p t) o -> p (t o)", t=PACK))
+        nc.sync.dma_start(xw[:], x_words[0].rearrange("p c r -> p (c r)").bitcast(I32))
+        nc.sync.dma_start(ww[:].bitcast(I32), w1_words[0].bitcast(I32))
+        nc.sync.dma_start(l1[:], n1)
+        nc.sync.dma_start(l2[:], n2)
+        nc.sync.dma_start(l4[:], n4)
+        nc.sync.dma_start(l3[:], n3)
+
+        nc.scalar.activation(gsc[:], gain[:], ACT.Copy, scale=0.0625 * 0.0625)
+
+        dsg = sb("dsg", [P, H], U8)
+        dsd = sb("dsd", [P, H], U8)
+        xsg = sb("xsg", [P, S], U8)
+        dwg = sb("dwg", [P, H], U32)
+        dwd = sb("dwd", [P, H], U32)
+        xwg = sb("xwg", [P, S], U32)
+        nc.vector.tensor_copy(dsg[:], ds[:].indirect(lk[:]))
+        nc.vector.tensor_copy(xsg[:], xs[:].indirect(lo[:]))
+        nc.vector.tensor_copy(
+            dsd[:].rearrange("p (t m) -> p m t", t=PACK), dsg[:].rearrange("p (m t) -> p m t", t=PACK)
+        )
+        for e in range(2):
+            nc.scalar.dma_start(dsd[2 + e : P : 32, :].bitcast(I32), dsd[16 + e : P : 32, :].bitcast(I32))
+        ws = sb("ws", [P, N], U8, tag="dsg")
+        nc.vector.memset(ws[:].bitcast(I32), 0)
+        w_rows = w1_scales[0].rearrange("(q r) c -> r q c", r=4)
+        for r in range(4):
+            nc.scalar.dma_start(ws[r:P:32, :].bitcast(I32), w_rows[r].bitcast(I32))
+        nc.vector.tensor_copy(dwg[:], dw[:].bitcast(U32).indirect(lk[:]))
+        nc.vector.tensor_copy(
+            dwd[:].bitcast(I32).rearrange("p (t m) -> p m t", t=PACK),
+            dwg[:].bitcast(I32).rearrange("p (m t) -> p m t", t=PACK),
+        )
+        nc.vector.tensor_copy(xwg[:], xw[:].bitcast(U32).indirect(lo[:]))
+
+        wwd = sb("wwd", [P, 2 * N], U8, tag="xw")
+        wsd = sb("wsd", [P, N], U8, tag="ww")
+        nc.vector.tensor_copy(
+            wwd[:].rearrange("p (t m b) -> p m t b", t=PACK, b=2), ww[:].rearrange("p (m t b) -> p m t b", t=PACK, b=2)
+        )
+        nc.vector.tensor_copy(
+            wsd[:].rearrange("p (t m) -> p m t", t=PACK), ws[:].rearrange("p (m t) -> p m t", t=PACK)
+        )
+
+        s_ps = [psum.tile([P, S], F32, name=f"s_ps{t}") for t in range(PACK)]
+        for t in range(PACK):
+            nc.tensor.matmul_mx(
+                out=s_ps[t][:],
+                lhsT=dwd[:, t * P : (t + 1) * P].bitcast(FP8X4),
+                lhsT_scale=dsd[:, t * P : (t + 1) * P],
+                rhs=xwg[:].bitcast(FP8X4),
+                rhs_scale=xsg[4:P, :],
+                start=True,
+                stop=True,
+            )
+        sa = [sb(f"sa{t}", [P, S], F32) for t in range(PACK)]
+        sg = [sb(f"sg{t}", [P, S], F32) for t in range(PACK)]
+        for pair in range(2):
+            for t in (2 * pair, 2 * pair + 1):
+                nc.scalar.copy(sa[t][:], s_ps[t][:])
+            for t in (2 * pair, 2 * pair + 1):
+                nc.scalar.activation(sg[t][:], s_ps[t][:], ACT.Copy, scale=gsc[:, t : t + 1])
+
+        ring = [sb(f"ring{i}", [P, 256], F32) for i in range(2)]
+        hw = [sb(f"hw{t}", [P, S], F32) for t in range(PACK)]
+        hp = []
+        last = len(CHUNKS) - 1
+        for c, (j0, w) in enumerate(CHUNKS):
+            z32 = sb(f"z32_{c}", [P, PACK * w], F32)
+            for pair in range(2):
+                for i in range(2):
+                    t = 2 * pair + i
+                    nc.vector.tensor_copy(ring[i][:, 0:w], sa[t][:].indirect(entries(l1, j0, w)))
+                for i in range(2):
+                    t = 2 * pair + i
+                    nc.vector.tensor_tensor(
+                        z32[:, t * w : (t + 1) * w], sg[t][:].indirect(entries(l2, j0, w)), ring[i][:, 0:w], ALU.mult
+                    )
+            zb = sb(f"zb{c}", [P, PACK * w], BF16)
+            zin = z32[:].rearrange("p (t j) -> p j t", t=PACK)
+            zout = zb[:].rearrange("p (j t) -> p j t", t=PACK)
+            if c == last:
+                nc.vector.tensor_copy(zout, zin)
+            else:
+                nc.scalar.copy(zout, zin)
+            zw = sb(f"zw{c}", [P, w], U32)
+            zs = sb(f"zs{c}", [P, w], U8)
+            nc.vector.quantize_mx(out=zw[:].bitcast(FP8X4), scales=zs[:], in_=zb[:])
+            per_bank = 512 // w
+            banks = [psum.tile([P, 512], F32, name=f"h_ps{c}_{b}") for b in range(PACK // per_bank)]
+            for t in range(PACK):
+                nc.tensor.matmul_mx(
+                    out=banks[t // per_bank][:, (t % per_bank) * w : (t % per_bank + 1) * w],
+                    lhsT=wwd[:, 2 * t * P : 2 * (t + 1) * P].bitcast(FP4X4),
+                    lhsT_scale=wsd[:, t * P : (t + 1) * P],
+                    rhs=zw[:].bitcast(FP8X4),
+                    rhs_scale=zs[:],
+                    start=True,
+                    stop=True,
+                )
+            for t in range(PACK):
+                nc.scalar.activation(
+                    hw[t][:, j0 : j0 + w],
+                    banks[t // per_bank][:, (t % per_bank) * w : (t % per_bank + 1) * w],
+                    ACT.Copy,
+                    scale=-1.0,
+                )
+            plain = sb(f"hp{c}", [P, PACK * w], F32)
+            for b in range(len(banks)):
+                nc.scalar.activation(plain[:, 512 * b : 512 * (b + 1)], banks[b][:], ACT.Copy, scale=-1.0)
+            hp.append(plain)
+
+        first = sb("first", [P, 1024], F32)
+        second = sb("second", [P, 1024], F32)
+        vbuf = [first[:, 0:1024], second[:, 0:512], second[:, 512:1024]]
+        ubuf = [second[:, 0:1024], second[:, 512:1024], second[:, 0:512]]
+        ow = sb("ow", [P, S], U32)
+        osc = sb("osc", [P, S], U8)
+        out_rows = out_0.rearrange("(p t) j -> p t j", t=PACK)
+        out_words = out_1[0].rearrange("p c r -> p (c r)").bitcast(I32)
+        for c, (j0, w) in enumerate(CHUNKS):
+            for t in range(PACK):
+                cols = slice(t * w, (t + 1) * w)
+                nc.vector.tensor_tensor(
+                    vbuf[c][:, cols], hw[t][:].indirect(entries(l4, j0, w)), hp[c][:, cols], ALU.subtract
+                )
+            half = sb(f"half{c}", [P, PACK * w], F32)
+            for pair in range(2):
+                cols = slice(2 * pair * w, 2 * (pair + 1) * w)
+                nc.scalar.activation(half[:, cols], vbuf[c][:, cols], ACT.Relu, scale=-0.5)
+            for t in range(PACK):
+                cols = slice(t * w, (t + 1) * w)
+                nc.vector.tensor_tensor(
+                    ubuf[c][:, cols], hw[t][:].indirect(entries(l3, j0, w)), hp[c][:, cols], ALU.subtract
+                )
+            o32 = sb(f"o32_{c}", [P, PACK * w], F32)
+            for pair in range(2):
+                cols = slice(2 * pair * w, 2 * (pair + 1) * w)
+                nc.vector.scalar_tensor_tensor(o32[:, cols], ubuf[c][:, cols], 0.0, half[:, cols], ALU.max, ALU.add)
+            nc.sync.dma_start(out_rows[:, :, j0 : j0 + w], o32[:].rearrange("p (t j) -> p t j", t=PACK))
+            ob = sb(f"ob{c}", [P, PACK * w], BF16)
+            oin = o32[:].rearrange("p (t j) -> p j t", t=PACK)
+            oout = ob[:].rearrange("p (j t) -> p j t", t=PACK)
+            if c == last:
+                nc.vector.tensor_copy(oout, oin)
+            else:
+                nc.scalar.copy(oout, oin)
+            nc.vector.quantize_mx(out=ow[:, j0 : j0 + w].bitcast(FP8X4), scales=osc[:, j0 : j0 + w], in_=ob[:])
+            nc.sync.dma_start(out_words[:, j0 : j0 + w], ow[:, j0 : j0 + w].bitcast(I32))
+        o_rows = out_2[0].rearrange("(q r) c -> r q c", r=4)
+        for r in range(4):
+            eng = nc.scalar if r % 2 else nc.sync
+            eng.dma_start(o_rows[r].bitcast(I32), osc[r:P:32, :].bitcast(I32))

@@ -49,63 +49,57 @@ def tile_picked_keyprodhinge_none_po_kernel(
         dw = sb("dw", [P, G], I32)
         xw = sb("xw", [P, T], I32)
         ww = sb("ww", [P, 2 * N], U8)
+        ws = sb("ws", [P, N], U8)
         gain = sb("gain", [P, PACK], F32)
-        gsc = sb("gsc", [P, PACK], F32)
 
         nc.vector.memset(ds[:].bitcast(I32), 0)
-        nc.vector.memset(xs[:].bitcast(I32), 0)
+        nc.gpsimd.memset(xs[:].bitcast(I32), 0)
+        nc.gpsimd.memset(ws[:].bitcast(I32), 0)
 
         nc.sync.dma_start(lk[:], kidx)
-        d_rows = d_scales[0].rearrange("(g e) c -> e g c", e=2)
-        for e in range(2):
-            nc.scalar.dma_start(ds[e:P:16, :].bitcast(I32), d_rows[e].bitcast(I32))
-        x_rows = x_scales[0].rearrange("(q r) c -> r q c", r=4)
-        for r in range(4):
-            nc.scalar.dma_start(xs[4 + r : P : 32, :].bitcast(I32), x_rows[r].bitcast(I32))
-        nc.sync.dma_start(dw[:], d_words[0].rearrange("p c r -> p (c r)").bitcast(I32))
         nc.sync.dma_start(lo[:], offs)
-        nc.sync.dma_start(gain[:], gn.rearrange("(p t) o -> p (t o)", t=PACK))
-        nc.sync.dma_start(xw[:], x_words[0].rearrange("p c r -> p (c r)").bitcast(I32))
-        nc.sync.dma_start(ww[:].bitcast(I32), w1_words[0].bitcast(I32))
+        nc.sync.dma_start(ds[0:P:8, :].bitcast(I32), d_scales[0].bitcast(I32))
         nc.sync.dma_start(l1[:], n1)
+        nc.sync.dma_start(xs[0:P:8, :].bitcast(I32), x_scales[0].bitcast(I32))
+        nc.scalar.dma_start(gain[:], gn.rearrange("(p t) o -> p (t o)", t=PACK))
+        nc.scalar.dma_start(ww[:].bitcast(I32), w1_words[0].bitcast(I32))
+        nc.sync.dma_start(dw[:], d_words[0].rearrange("p c r -> p (c r)").bitcast(I32))
+        nc.sync.dma_start(xw[:], x_words[0].rearrange("p c r -> p (c r)").bitcast(I32))
         nc.sync.dma_start(l2[:], n2)
         nc.sync.dma_start(l4[:], n4)
         nc.sync.dma_start(l3[:], n3)
-
-        nc.scalar.activation(gsc[:], gain[:], ACT.Copy, scale=0.0625 * 0.0625)
+        w_rows = w1_scales[0].rearrange("(q r) c -> r q c", r=4)
+        for r in range(4):
+            nc.gpsimd.dma_start(ws[r:P:32, :].bitcast(I32), w_rows[r].bitcast(I32))
 
         dsg = sb("dsg", [P, H], U8)
-        dsd = sb("dsd", [P, H], U8)
         xsg = sb("xsg", [P, S], U8)
+        planes = sb("planes", [P, H + S], U8)
         dwg = sb("dwg", [P, H], U32)
         dwd = sb("dwd", [P, H], U32)
         xwg = sb("xwg", [P, S], U32)
         nc.vector.tensor_copy(dsg[:], ds[:].indirect(lk[:]))
         nc.vector.tensor_copy(xsg[:], xs[:].indirect(lo[:]))
         nc.vector.tensor_copy(
-            dsd[:].rearrange("p (t m) -> p m t", t=PACK), dsg[:].rearrange("p (m t) -> p m t", t=PACK)
+            planes[:, 0:H].rearrange("p (t m) -> p t m", t=PACK), dsg[:].rearrange("p (m t) -> p t m", t=PACK)
         )
-        for e in range(2):
-            nc.scalar.dma_start(dsd[2 + e : P : 32, :].bitcast(I32), dsd[16 + e : P : 32, :].bitcast(I32))
-        ws = sb("ws", [P, N], U8, tag="dsg")
-        nc.vector.memset(ws[:].bitcast(I32), 0)
-        w_rows = w1_scales[0].rearrange("(q r) c -> r q c", r=4)
-        for r in range(4):
-            nc.scalar.dma_start(ws[r:P:32, :].bitcast(I32), w_rows[r].bitcast(I32))
+        nc.vector.tensor_copy(planes[:, H : H + S].bitcast(I32), xsg[:].bitcast(I32))
+        for r in range(1, 4):
+            nc.scalar.dma_start(planes[r:P:32, :].bitcast(I32), planes[8 * r : P : 32, :].bitcast(I32))
         nc.vector.tensor_copy(dwg[:], dw[:].bitcast(U32).indirect(lk[:]))
         nc.vector.tensor_copy(
-            dwd[:].bitcast(I32).rearrange("p (t m) -> p m t", t=PACK),
-            dwg[:].bitcast(I32).rearrange("p (m t) -> p m t", t=PACK),
+            dwd[:].bitcast(I32).rearrange("p (t b i) -> p b t i", t=PACK, i=4),
+            dwg[:].bitcast(I32).rearrange("p (b i t) -> p b t i", t=PACK, i=4),
         )
         nc.vector.tensor_copy(xwg[:], xw[:].bitcast(U32).indirect(lo[:]))
 
         wwd = sb("wwd", [P, 2 * N], U8, tag="xw")
         wsd = sb("wsd", [P, N], U8, tag="ww")
         nc.vector.tensor_copy(
-            wwd[:].rearrange("p (t m b) -> p m t b", t=PACK, b=2), ww[:].rearrange("p (m t b) -> p m t b", t=PACK, b=2)
+            wwd[:].rearrange("p (t m b) -> p t m b", t=PACK, b=2), ww[:].rearrange("p (m t b) -> p t m b", t=PACK, b=2)
         )
         nc.vector.tensor_copy(
-            wsd[:].rearrange("p (t m) -> p m t", t=PACK), ws[:].rearrange("p (m t) -> p m t", t=PACK)
+            wsd[:].rearrange("p (t m) -> p t m", t=PACK), ws[:].rearrange("p (m t) -> p t m", t=PACK)
         )
 
         s_ps = [psum.tile([P, S], F32, name=f"s_ps{t}") for t in range(PACK)]
@@ -113,9 +107,9 @@ def tile_picked_keyprodhinge_none_po_kernel(
             nc.tensor.matmul_mx(
                 out=s_ps[t][:],
                 lhsT=dwd[:, t * P : (t + 1) * P].bitcast(FP8X4),
-                lhsT_scale=dsd[:, t * P : (t + 1) * P],
+                lhsT_scale=planes[:, t * P : (t + 1) * P],
                 rhs=xwg[:].bitcast(FP8X4),
-                rhs_scale=xsg[4:P, :],
+                rhs_scale=planes[:, H : H + S],
                 start=True,
                 stop=True,
             )
@@ -123,9 +117,9 @@ def tile_picked_keyprodhinge_none_po_kernel(
         sg = [sb(f"sg{t}", [P, S], F32) for t in range(PACK)]
         for pair in range(2):
             for t in (2 * pair, 2 * pair + 1):
-                nc.scalar.copy(sa[t][:], s_ps[t][:])
+                nc.scalar.activation(sa[t][:], s_ps[t][:], ACT.Copy, scale=0.0625 * 0.0625)
             for t in (2 * pair, 2 * pair + 1):
-                nc.scalar.activation(sg[t][:], s_ps[t][:], ACT.Copy, scale=gsc[:, t : t + 1])
+                nc.scalar.activation(sg[t][:], s_ps[t][:], ACT.Copy, scale=gain[:, t : t + 1])
 
         ring = [sb(f"ring{i}", [P, 256], F32) for i in range(2)]
         hw = [sb(f"hw{t}", [P, S], F32) for t in range(PACK)]

@@ -1,6 +1,7 @@
 from contextlib import ExitStack
 
 import concourse.mybir as mybir
+from concourse.masks import make_identity
 
 K, T, S, N, G, H = 512, 2048, 512, 512, 2048, 512
 FLOPS = 2 * K * H * S + 2 * H * N * S
@@ -53,8 +54,14 @@ def tile_picked_keyprodhinge_none_po_kernel(
         gain = sb("gain", [P, PACK], F32)
 
         nc.vector.memset(ds[:].bitcast(I32), 0)
-        nc.gpsimd.memset(xs[:].bitcast(I32), 0)
-        nc.gpsimd.memset(ws[:].bitcast(I32), 0)
+        nc.vector.memset(xs[:].bitcast(I32), 0)
+        nc.vector.memset(ws[:].bitcast(I32), 0)
+        ident = sb("ident", [P, P], F32)
+        nc.vector.memset(ident[:], 0.0)
+        make_identity(nc, ident[:], nomemset=True)
+        wide = [sb(f"wide{t}", [P, 2 * S], F32) for t in range(PACK)]
+        for t in range(2):
+            nc.vector.memset(wide[t][:, S : 2 * S], 0.0)
 
         nc.sync.dma_start(lk[:], kidx)
         nc.sync.dma_start(lo[:], offs)
@@ -91,7 +98,8 @@ def tile_picked_keyprodhinge_none_po_kernel(
             dwd[:].bitcast(I32).rearrange("p (t b i) -> p b t i", t=PACK, i=4),
             dwg[:].bitcast(I32).rearrange("p (b i t) -> p b t i", t=PACK, i=4),
         )
-        nc.vector.tensor_copy(xwg[:], xw[:].bitcast(U32).indirect(lo[:]))
+        for j0 in (0, S // 2):
+            nc.vector.tensor_copy(xwg[:, j0 : j0 + S // 2], xw[:].bitcast(U32).indirect(entries(lo, j0, S // 2)))
 
         wwd = sb("wwd", [P, 2 * N], U8, tag="xw")
         wsd = sb("wsd", [P, N], U8, tag="ww")
@@ -102,55 +110,91 @@ def tile_picked_keyprodhinge_none_po_kernel(
             wsd[:].rearrange("p (t m) -> p t m", t=PACK), ws[:].rearrange("p (m t) -> p t m", t=PACK)
         )
 
-        s_ps = [psum.tile([P, S], F32, name=f"s_ps{t}") for t in range(PACK)]
-        for t in range(PACK):
+        pieces = [((0, S // 2), (S // 2, S // 2)) if t < 2 else ((0, S),) for t in range(PACK)]
+        s_ps = {}
+        for t, k in ((0, 0), (1, 0), (0, 1), (1, 1), (2, 0), (3, 0)):
+            j0, w = pieces[t][k]
+            s_ps[t, k] = psum.tile([P, w], F32, name=f"s_ps{t}_{k}")
             nc.tensor.matmul_mx(
-                out=s_ps[t][:],
+                out=s_ps[t, k][:],
                 lhsT=dwd[:, t * P : (t + 1) * P].bitcast(FP8X4),
                 lhsT_scale=planes[:, t * P : (t + 1) * P],
-                rhs=xwg[:].bitcast(FP8X4),
-                rhs_scale=planes[:, H : H + S],
+                rhs=xwg[:, j0 : j0 + w].bitcast(FP8X4),
+                rhs_scale=planes[:, H + j0 : H + j0 + w],
                 start=True,
                 stop=True,
             )
         sa = [sb(f"sa{t}", [P, S], F32) for t in range(PACK)]
         sg = [sb(f"sg{t}", [P, S], F32) for t in range(PACK)]
         for pair in range(2):
-            for t in (2 * pair, 2 * pair + 1):
-                nc.scalar.activation(sa[t][:], s_ps[t][:], ACT.Copy, scale=0.0625 * 0.0625)
-            for t in (2 * pair, 2 * pair + 1):
-                nc.scalar.activation(sg[t][:], s_ps[t][:], ACT.Copy, scale=gain[:, t : t + 1])
+            rows = (2 * pair, 2 * pair + 1)
+            for k in range(len(pieces[rows[0]])):
+                for t in rows:
+                    j0, w = pieces[t][k]
+                    nc.scalar.activation(sa[t][:, j0 : j0 + w], s_ps[t, k][:], ACT.Copy, scale=0.0625 * 0.0625)
+            for t in rows:
+                for k, (j0, w) in enumerate(pieces[t]):
+                    nc.scalar.activation(sg[t][:, j0 : j0 + w], s_ps[t, k][:], ACT.Copy, scale=gain[:, t : t + 1])
 
-        ring = [sb(f"ring{i}", [P, 256], F32) for i in range(2)]
-        hw = [sb(f"hw{t}", [P, S], F32) for t in range(PACK)]
-        hp = []
+        w0 = CHUNKS[0][1]
+        rest = S - w0
         last = len(CHUNKS) - 1
+        s1_first = [sb(f"s1_first{t}", [P, w0], F32, tag="late" if t == PACK - 1 else None) for t in range(PACK)]
+        z_first = sb("z_first", [P, PACK * w0], F32)
+
+        def product(dst, t, j0, w, src):
+            nc.vector.tensor_tensor(dst[:, t * w : (t + 1) * w], sg[t][:].indirect(entries(l2, j0, w)), src, ALU.mult)
+
+        for pair in range(2):
+            for t in (2 * pair, 2 * pair + 1):
+                nc.vector.tensor_copy(s1_first[t][:], sa[t][:].indirect(entries(l1, 0, w0)))
+            for t in (2 * pair, 2 * pair + 1):
+                product(z_first, t, 0, w0, s1_first[t][:])
+        s1_rest = sb("s1_rest", [P, PACK * rest], F32, tag="late")
+        hn = [sb(f"hn{t}", [P, 2 * S if t < 2 else S], F32) for t in range(PACK)]
+        sums = []
+
+        def negate(c, t):
+            j0, w = CHUNKS[c]
+            nc.scalar.activation(wide[t][:, j0 : j0 + w], sums[c][t], ACT.Copy, scale=-1.0)
+            nc.scalar.activation(hn[t][:, j0 : j0 + w], sums[c][t], ACT.Copy, scale=-1.0)
+
         for c, (j0, w) in enumerate(CHUNKS):
-            z32 = sb(f"z32_{c}", [P, PACK * w], F32)
-            for pair in range(2):
-                for i in range(2):
-                    t = 2 * pair + i
-                    nc.vector.tensor_copy(ring[i][:, 0:w], sa[t][:].indirect(entries(l1, j0, w)))
-                for i in range(2):
-                    t = 2 * pair + i
-                    nc.vector.tensor_tensor(
-                        z32[:, t * w : (t + 1) * w], sg[t][:].indirect(entries(l2, j0, w)), ring[i][:, 0:w], ALU.mult
-                    )
-            zb = sb(f"zb{c}", [P, PACK * w], BF16)
-            zin = z32[:].rearrange("p (t j) -> p j t", t=PACK)
+            if c == 0:
+                z32 = z_first[:]
+            else:
+                if c == 1:
+                    z_late = sb("z_late", [P, PACK * rest], F32, tag="zb0")
+                    for t in range(PACK):
+                        nc.vector.tensor_copy(
+                            s1_rest[:, t * rest : (t + 1) * rest], sa[t][:].indirect(entries(l1, w0, rest))
+                        )
+                z32 = z_late[:, PACK * (j0 - w0) : PACK * (j0 - w0 + w)]
+                for t in range(PACK):
+                    product(z32, t, j0, w, s1_rest[:, t * rest + j0 - w0 : t * rest + j0 - w0 + w])
+            zb = sb(f"zb{c}", [P, PACK * w], BF16, tag=f"zb{min(c, 1)}")
+            zin = z32.rearrange("p (t j) -> p j t", t=PACK)
             zout = zb[:].rearrange("p (j t) -> p j t", t=PACK)
             if c == last:
                 nc.vector.tensor_copy(zout, zin)
             else:
                 nc.scalar.copy(zout, zin)
+            if c == 1:
+                for t in range(PACK):
+                    negate(0, t)
             zw = sb(f"zw{c}", [P, w], U32)
             zs = sb(f"zs{c}", [P, w], U8)
             nc.vector.quantize_mx(out=zw[:].bitcast(FP8X4), scales=zs[:], in_=zb[:])
-            per_bank = 512 // w
-            banks = [psum.tile([P, 512], F32, name=f"h_ps{c}_{b}") for b in range(PACK // per_bank)]
+            if c == last:
+                banks = [psum.tile([P, S], F32, name=f"h_last{t}", tag=f"s_ps{t}_0") for t in range(PACK)]
+                h_ps = [banks[t][:, 0:w] for t in range(PACK)]
+            else:
+                per_bank = 512 // w
+                banks = [psum.tile([P, 512], F32, name=f"h_ps{c}_{b}", tag=("s_ps0_1", "s_ps1_1")[b] if c == 0 else "h_ps1_0") for b in range(PACK // per_bank)]
+                h_ps = [banks[t // per_bank][:, (t % per_bank) * w : (t % per_bank + 1) * w] for t in range(PACK)]
             for t in range(PACK):
                 nc.tensor.matmul_mx(
-                    out=banks[t // per_bank][:, (t % per_bank) * w : (t % per_bank + 1) * w],
+                    out=h_ps[t],
                     lhsT=wwd[:, 2 * t * P : 2 * (t + 1) * P].bitcast(FP4X4),
                     lhsT_scale=wsd[:, t * P : (t + 1) * P],
                     rhs=zw[:].bitcast(FP8X4),
@@ -158,54 +202,86 @@ def tile_picked_keyprodhinge_none_po_kernel(
                     start=True,
                     stop=True,
                 )
-            for t in range(PACK):
-                nc.scalar.activation(
-                    hw[t][:, j0 : j0 + w],
-                    banks[t // per_bank][:, (t % per_bank) * w : (t % per_bank + 1) * w],
-                    ACT.Copy,
-                    scale=-1.0,
-                )
-            plain = sb(f"hp{c}", [P, PACK * w], F32)
-            for b in range(len(banks)):
-                nc.scalar.activation(plain[:, 512 * b : 512 * (b + 1)], banks[b][:], ACT.Copy, scale=-1.0)
-            hp.append(plain)
+            sums.append(h_ps)
+        for t in range(PACK):
+            for c in range(1, len(CHUNKS)):
+                negate(c, t)
 
-        first = sb("first", [P, 1024], F32)
-        second = sb("second", [P, 1024], F32)
-        vbuf = [first[:, 0:1024], second[:, 0:512], second[:, 512:1024]]
-        ubuf = [second[:, 0:1024], second[:, 512:1024], second[:, 0:512]]
-        ow = sb("ow", [P, S], U32)
         osc = sb("osc", [P, S], U8)
         out_rows = out_0.rearrange("(p t) j -> p t j", t=PACK)
         out_words = out_1[0].rearrange("p c r -> p (c r)").bitcast(I32)
+        ob = [sb(f"ob{c}", [P, PACK * w], BF16) for c, (j0, w) in enumerate(CHUNKS)]
+
+        def blocks(tile, base=0):
+            return [tile[:, base + b * P : base + (b + 1) * P] for b in range(S // P)]
+
+        o_lo = sb("o_lo", [P, 2 * S], F32)
+        for t in range(2):
+            nc.vector.tensor_tensor(hn[t][:, S : 2 * S], wide[t][:].indirect(l4[:]), hn[t][:, 0:S], ALU.subtract)
+        for t in range(2):
+            nc.vector.tensor_tensor(
+                wide[2 + t][:, S : 2 * S], hn[t][:].indirect(l3[:]), wide[t][:, 0:S], ALU.subtract
+            )
+        turned = []
+        for k, (src, scale) in enumerate([(blocks(hn[0], S), -0.5), (blocks(wide[2], S), 1.0)]):
+            bank = psum.tile([P, S], F32, name=f"turn{k}", tag=f"s_ps{k}_1")
+            for b, dst in enumerate(blocks(bank)):
+                nc.tensor.transpose(dst, src[b], ident[:])
+            turned.append(sb(f"turned{k}", [P, S], F32))
+            nc.scalar.activation(turned[k][:], bank[:], ACT.Relu, scale=scale)
+            if k == 0:
+                half_lo = sb("half_lo", [P, S], F32)
+                nc.scalar.activation(half_lo[:], hn[1][:, S : 2 * S], ACT.Relu, scale=-0.5)
+        back = psum.tile([P, S], F32, name="back", tag="h_ps1_0")
+        for b, dst in enumerate(blocks(back)):
+            nc.tensor.matmul(dst, blocks(turned[0])[b], ident[:], is_transpose=True, start=True, stop=False)
+            nc.tensor.matmul(dst, blocks(turned[1])[b], ident[:], is_transpose=True, start=False, stop=True)
+        nc.scalar.copy(o_lo[:, 0:S], back[:])
+
+        up = sb("up", [P, 2 * S], F32)
+        down = sb("down", [P, 2 * w0], F32)
+        half = [sb(f"half{c}", [P, 2 * w], F32) for c, (j0, w) in enumerate(CHUNKS)]
+        for i in range(2):
+            nc.vector.tensor_tensor(up[:, i * S : (i + 1) * S], wide[2 + i][:].indirect(l4[:]), hn[2 + i][:], ALU.subtract)
+            for c, (j0, w) in enumerate(CHUNKS):
+                nc.scalar.activation(
+                    half[c][:, i * w : (i + 1) * w], up[:, i * S + j0 : i * S + j0 + w], ACT.Relu, scale=-0.5
+                )
+            if i == 0:
+                nc.vector.scalar_tensor_tensor(
+                    o_lo[:, S : 2 * S], wide[3][:, S : 2 * S], 0.0, half_lo[:], ALU.max, ALU.add
+                )
+                nc.sync.dma_start(out_rows[:, 0:2, :], o_lo[:].rearrange("p (t j) -> p t j", t=2))
         for c, (j0, w) in enumerate(CHUNKS):
-            for t in range(PACK):
-                cols = slice(t * w, (t + 1) * w)
+            nc.scalar.copy(
+                ob[c][:].rearrange("p (j t) -> p j t", t=PACK)[:, :, 0:2],
+                o_lo[:].rearrange("p (t j) -> p j t", t=2)[:, j0 : j0 + w, :],
+            )
+        for c, (j0, w) in enumerate(CHUNKS):
+            for i in range(2):
                 nc.vector.tensor_tensor(
-                    vbuf[c][:, cols], hw[t][:].indirect(entries(l4, j0, w)), hp[c][:, cols], ALU.subtract
+                    down[:, i * w0 : i * w0 + w],
+                    hn[2 + i][:].indirect(entries(l3, j0, w)),
+                    wide[2 + i][:, j0 : j0 + w],
+                    ALU.subtract,
                 )
-            half = sb(f"half{c}", [P, PACK * w], F32)
-            for pair in range(2):
-                cols = slice(2 * pair * w, 2 * (pair + 1) * w)
-                nc.scalar.activation(half[:, cols], vbuf[c][:, cols], ACT.Relu, scale=-0.5)
-            for t in range(PACK):
-                cols = slice(t * w, (t + 1) * w)
-                nc.vector.tensor_tensor(
-                    ubuf[c][:, cols], hw[t][:].indirect(entries(l3, j0, w)), hp[c][:, cols], ALU.subtract
+            o_hi = sb(f"o_hi{c}", [P, 2 * w], F32)
+            for i in range(2):
+                cols = slice(i * w, (i + 1) * w)
+                nc.vector.scalar_tensor_tensor(
+                    o_hi[:, cols], down[:, i * w0 : i * w0 + w], 0.0, half[c][:, cols], ALU.max, ALU.add
                 )
-            o32 = sb(f"o32_{c}", [P, PACK * w], F32)
-            for pair in range(2):
-                cols = slice(2 * pair * w, 2 * (pair + 1) * w)
-                nc.vector.scalar_tensor_tensor(o32[:, cols], ubuf[c][:, cols], 0.0, half[:, cols], ALU.max, ALU.add)
-            nc.sync.dma_start(out_rows[:, :, j0 : j0 + w], o32[:].rearrange("p (t j) -> p t j", t=PACK))
-            ob = sb(f"ob{c}", [P, PACK * w], BF16)
-            oin = o32[:].rearrange("p (t j) -> p j t", t=PACK)
-            oout = ob[:].rearrange("p (j t) -> p j t", t=PACK)
+            nc.sync.dma_start(out_rows[:, 2:4, j0 : j0 + w], o_hi[:].rearrange("p (t j) -> p t j", t=2))
+            if c == last:
+                ow = sb("ow", [P, S], U32, tag="half1")
+            oin = o_hi[:].rearrange("p (t j) -> p j t", t=2)
+            oout = ob[c][:].rearrange("p (j t) -> p j t", t=PACK)[:, :, 2:4]
             if c == last:
                 nc.vector.tensor_copy(oout, oin)
             else:
                 nc.scalar.copy(oout, oin)
-            nc.vector.quantize_mx(out=ow[:, j0 : j0 + w].bitcast(FP8X4), scales=osc[:, j0 : j0 + w], in_=ob[:])
+        for c, (j0, w) in enumerate(CHUNKS):
+            nc.vector.quantize_mx(out=ow[:, j0 : j0 + w].bitcast(FP8X4), scales=osc[:, j0 : j0 + w], in_=ob[c][:])
             nc.sync.dma_start(out_words[:, j0 : j0 + w], ow[:, j0 : j0 + w].bitcast(I32))
         o_rows = out_2[0].rearrange("(q r) c -> r q c", r=4)
         for r in range(4):

from contextlib import ExitStack

import concourse.mybir as mybir
from concourse.masks import make_identity

K, T, S, N, G, H = 512, 2048, 512, 512, 2048, 512
FLOPS = 2 * K * H * S + 2 * H * N * S

F32 = mybir.dt.float32
BF16 = mybir.dt.bfloat16
I32 = mybir.dt.int32
U32 = mybir.dt.uint32
U16 = mybir.dt.uint16
U8 = mybir.dt.uint8
FP8X4 = mybir.dt.float8_e4m3fn_x4
FP4X4 = mybir.dt.float4_e2m1fn_x4
ALU = mybir.AluOpType
ACT = mybir.ActivationFunctionType

P = 128
PACK = 4
CHUNKS = ((0, 256), (256, 128), (384, 128))


def entries(lst, start, width):
    return lst[:, start // 16 : (start + width) // 16]


def tile_picked_keyprodhinge_none_po_kernel(
    tc, x_words, x_scales, d_words, d_scales, gn, w1_words, w1_scales, offs, kidx, n1, n2, n3, n4, out_0, out_1, out_2
):
    nc = tc.nc
    with ExitStack() as ctx:
        lists = ctx.enter_context(tc.tile_pool(name="lists", bufs=1))
        keep = ctx.enter_context(tc.tile_pool(name="keep", bufs=1))
        psum = ctx.enter_context(tc.psum_pool(name="psum", bufs=1))

        def sb(name, shape, dtype, tag=None):
            return keep.tile(shape, dtype, name=name, tag=tag or name, align_bytes=64)

        lk = lists.tile([P, H // 16], U16, name="lk")
        lo = lists.tile([P, S // 16], U16, name="lo")
        l1 = lists.tile([P, S // 16], U16, name="l1")
        l2 = lists.tile([P, S // 16], U16, name="l2")
        l3 = lists.tile([P, S // 16], U16, name="l3")
        l4 = lists.tile([P, S // 16], U16, name="l4")

        ds = sb("ds", [P, G], U8)
        xs = sb("xs", [P, T], U8)
        dw = sb("dw", [P, G], I32)
        xw = sb("xw", [P, T], I32)
        ww = sb("ww", [P, 2 * N], U8)
        ws = sb("ws", [P, N], U8)
        gain = sb("gain", [P, PACK], F32)

        nc.vector.memset(ds[:].bitcast(I32), 0)
        nc.vector.memset(xs[:].bitcast(I32), 0)
        nc.vector.memset(ws[:].bitcast(I32), 0)
        ident = sb("ident", [P, P], F32)
        nc.vector.memset(ident[:], 0.0)
        make_identity(nc, ident[:], nomemset=True)
        wide = [sb(f"wide{t}", [P, 2 * S], F32) for t in range(PACK)]
        for t in range(2):
            nc.vector.memset(wide[t][:, S : 2 * S], 0.0)

        nc.sync.dma_start(lk[:], kidx)
        nc.sync.dma_start(lo[:], offs)
        nc.sync.dma_start(ds[0:P:8, :].bitcast(I32), d_scales[0].bitcast(I32))
        nc.sync.dma_start(l1[:], n1)
        nc.sync.dma_start(xs[0:P:8, :].bitcast(I32), x_scales[0].bitcast(I32))
        nc.scalar.dma_start(gain[:], gn.rearrange("(p t) o -> p (t o)", t=PACK))
        nc.scalar.dma_start(ww[:].bitcast(I32), w1_words[0].bitcast(I32))
        nc.sync.dma_start(dw[:], d_words[0].rearrange("p c r -> p (c r)").bitcast(I32))
        nc.sync.dma_start(xw[:], x_words[0].rearrange("p c r -> p (c r)").bitcast(I32))
        nc.sync.dma_start(l2[:], n2)
        nc.sync.dma_start(l4[:], n4)
        nc.sync.dma_start(l3[:], n3)
        w_rows = w1_scales[0].rearrange("(q r) c -> r q c", r=4)
        for r in range(4):
            nc.gpsimd.dma_start(ws[r:P:32, :].bitcast(I32), w_rows[r].bitcast(I32))

        dsg = sb("dsg", [P, H], U8)
        xsg = sb("xsg", [P, S], U8)
        planes = sb("planes", [P, H + S], U8)
        dwg = sb("dwg", [P, H], U32)
        dwd = sb("dwd", [P, H], U32)
        xwg = sb("xwg", [P, S], U32)
        nc.vector.tensor_copy(dsg[:], ds[:].indirect(lk[:]))
        nc.vector.tensor_copy(xsg[:], xs[:].indirect(lo[:]))
        nc.vector.tensor_copy(
            planes[:, 0:H].rearrange("p (t m) -> p t m", t=PACK), dsg[:].rearrange("p (m t) -> p t m", t=PACK)
        )
        nc.vector.tensor_copy(planes[:, H : H + S].bitcast(I32), xsg[:].bitcast(I32))
        for r in range(1, 4):
            nc.scalar.dma_start(planes[r:P:32, :].bitcast(I32), planes[8 * r : P : 32, :].bitcast(I32))
        nc.vector.tensor_copy(dwg[:], dw[:].bitcast(U32).indirect(lk[:]))
        nc.vector.tensor_copy(
            dwd[:].bitcast(I32).rearrange("p (t b i) -> p b t i", t=PACK, i=4),
            dwg[:].bitcast(I32).rearrange("p (b i t) -> p b t i", t=PACK, i=4),
        )
        for j0 in (0, S // 2):
            nc.vector.tensor_copy(xwg[:, j0 : j0 + S // 2], xw[:].bitcast(U32).indirect(entries(lo, j0, S // 2)))

        wwd = sb("wwd", [P, 2 * N], U8, tag="xw")
        wsd = sb("wsd", [P, N], U8, tag="ww")
        nc.vector.tensor_copy(
            wwd[:].rearrange("p (t m b) -> p t m b", t=PACK, b=2), ww[:].rearrange("p (m t b) -> p t m b", t=PACK, b=2)
        )
        nc.vector.tensor_copy(
            wsd[:].rearrange("p (t m) -> p t m", t=PACK), ws[:].rearrange("p (m t) -> p t m", t=PACK)
        )

        pieces = [((0, S // 2), (S // 2, S // 2)) if t < 2 else ((0, S),) for t in range(PACK)]
        s_ps = {}
        for t, k in ((0, 0), (1, 0), (0, 1), (1, 1), (2, 0), (3, 0)):
            j0, w = pieces[t][k]
            s_ps[t, k] = psum.tile([P, w], F32, name=f"s_ps{t}_{k}")
            nc.tensor.matmul_mx(
                out=s_ps[t, k][:],
                lhsT=dwd[:, t * P : (t + 1) * P].bitcast(FP8X4),
                lhsT_scale=planes[:, t * P : (t + 1) * P],
                rhs=xwg[:, j0 : j0 + w].bitcast(FP8X4),
                rhs_scale=planes[:, H + j0 : H + j0 + w],
                start=True,
                stop=True,
            )
        sa = [sb(f"sa{t}", [P, S], F32) for t in range(PACK)]
        sg = [sb(f"sg{t}", [P, S], F32) for t in range(PACK)]
        for pair in range(2):
            rows = (2 * pair, 2 * pair + 1)
            for k in range(len(pieces[rows[0]])):
                for t in rows:
                    j0, w = pieces[t][k]
                    nc.scalar.activation(sa[t][:, j0 : j0 + w], s_ps[t, k][:], ACT.Copy, scale=0.0625 * 0.0625)
            for t in rows:
                for k, (j0, w) in enumerate(pieces[t]):
                    nc.scalar.activation(sg[t][:, j0 : j0 + w], s_ps[t, k][:], ACT.Copy, scale=gain[:, t : t + 1])

        w0 = CHUNKS[0][1]
        rest = S - w0
        last = len(CHUNKS) - 1
        s1_first = [sb(f"s1_first{t}", [P, w0], F32, tag="late" if t == PACK - 1 else None) for t in range(PACK)]
        z_first = sb("z_first", [P, PACK * w0], F32)

        def product(dst, t, j0, w, src):
            nc.vector.tensor_tensor(dst[:, t * w : (t + 1) * w], sg[t][:].indirect(entries(l2, j0, w)), src, ALU.mult)

        for pair in range(2):
            for t in (2 * pair, 2 * pair + 1):
                nc.vector.tensor_copy(s1_first[t][:], sa[t][:].indirect(entries(l1, 0, w0)))
            for t in (2 * pair, 2 * pair + 1):
                product(z_first, t, 0, w0, s1_first[t][:])
        s1_rest = sb("s1_rest", [P, PACK * rest], F32, tag="late")
        hn = [sb(f"hn{t}", [P, 2 * S if t < 2 else S], F32) for t in range(PACK)]
        sums = []

        def negate(c, t):
            j0, w = CHUNKS[c]
            nc.scalar.activation(wide[t][:, j0 : j0 + w], sums[c][t], ACT.Copy, scale=-1.0)
            nc.scalar.activation(hn[t][:, j0 : j0 + w], sums[c][t], ACT.Copy, scale=-1.0)

        for c, (j0, w) in enumerate(CHUNKS):
            if c == 0:
                z32 = z_first[:]
            else:
                if c == 1:
                    z_late = sb("z_late", [P, PACK * rest], F32, tag="zb0")
                    for t in range(PACK):
                        nc.vector.tensor_copy(
                            s1_rest[:, t * rest : (t + 1) * rest], sa[t][:].indirect(entries(l1, w0, rest))
                        )
                z32 = z_late[:, PACK * (j0 - w0) : PACK * (j0 - w0 + w)]
                for t in range(PACK):
                    product(z32, t, j0, w, s1_rest[:, t * rest + j0 - w0 : t * rest + j0 - w0 + w])
            zb = sb(f"zb{c}", [P, PACK * w], BF16, tag=f"zb{min(c, 1)}")
            zin = z32.rearrange("p (t j) -> p j t", t=PACK)
            zout = zb[:].rearrange("p (j t) -> p j t", t=PACK)
            if c == last:
                nc.vector.tensor_copy(zout, zin)
            else:
                nc.scalar.copy(zout, zin)
            if c == 1:
                for t in range(PACK):
                    negate(0, t)
            zw = sb(f"zw{c}", [P, w], U32)
            zs = sb(f"zs{c}", [P, w], U8)
            nc.vector.quantize_mx(out=zw[:].bitcast(FP8X4), scales=zs[:], in_=zb[:])
            if c == last:
                banks = [psum.tile([P, S], F32, name=f"h_last{t}", tag=f"s_ps{t}_0") for t in range(PACK)]
                h_ps = [banks[t][:, 0:w] for t in range(PACK)]
            else:
                per_bank = 512 // w
                banks = [psum.tile([P, 512], F32, name=f"h_ps{c}_{b}", tag=("s_ps0_1", "s_ps1_1")[b] if c == 0 else "h_ps1_0") for b in range(PACK // per_bank)]
                h_ps = [banks[t // per_bank][:, (t % per_bank) * w : (t % per_bank + 1) * w] for t in range(PACK)]
            for t in range(PACK):
                nc.tensor.matmul_mx(
                    out=h_ps[t],
                    lhsT=wwd[:, 2 * t * P : 2 * (t + 1) * P].bitcast(FP4X4),
                    lhsT_scale=wsd[:, t * P : (t + 1) * P],
                    rhs=zw[:].bitcast(FP8X4),
                    rhs_scale=zs[:],
                    start=True,
                    stop=True,
                )
            sums.append(h_ps)
        for t in range(PACK):
            for c in range(1, len(CHUNKS)):
                negate(c, t)

        osc = sb("osc", [P, S], U8)
        out_rows = out_0.rearrange("(p t) j -> p t j", t=PACK)
        out_words = out_1[0].rearrange("p c r -> p (c r)").bitcast(I32)
        ob = [sb(f"ob{c}", [P, PACK * w], BF16) for c, (j0, w) in enumerate(CHUNKS)]

        def blocks(tile, base=0):
            return [tile[:, base + b * P : base + (b + 1) * P] for b in range(S // P)]

        o_lo = sb("o_lo", [P, 2 * S], F32)
        for t in range(2):
            nc.vector.tensor_tensor(hn[t][:, S : 2 * S], wide[t][:].indirect(l4[:]), hn[t][:, 0:S], ALU.subtract)
        for t in range(2):
            nc.vector.tensor_tensor(
                wide[2 + t][:, S : 2 * S], hn[t][:].indirect(l3[:]), wide[t][:, 0:S], ALU.subtract
            )
        turned = []
        for k, (src, scale) in enumerate([(blocks(hn[0], S), -0.5), (blocks(wide[2], S), 1.0)]):
            bank = psum.tile([P, S], F32, name=f"turn{k}", tag=f"s_ps{k}_1")
            for b, dst in enumerate(blocks(bank)):
                nc.tensor.transpose(dst, src[b], ident[:])
            turned.append(sb(f"turned{k}", [P, S], F32))
            nc.scalar.activation(turned[k][:], bank[:], ACT.Relu, scale=scale)
            if k == 0:
                half_lo = sb("half_lo", [P, S], F32)
                nc.scalar.activation(half_lo[:], hn[1][:, S : 2 * S], ACT.Relu, scale=-0.5)
        back = psum.tile([P, S], F32, name="back", tag="h_ps1_0")
        for b, dst in enumerate(blocks(back)):
            nc.tensor.matmul(dst, blocks(turned[0])[b], ident[:], is_transpose=True, start=True, stop=False)
            nc.tensor.matmul(dst, blocks(turned[1])[b], ident[:], is_transpose=True, start=False, stop=True)
        nc.scalar.copy(o_lo[:, 0:S], back[:])

        up = sb("up", [P, 2 * S], F32)
        down = sb("down", [P, 2 * w0], F32)
        half = [sb(f"half{c}", [P, 2 * w], F32) for c, (j0, w) in enumerate(CHUNKS)]
        for i in range(2):
            nc.vector.tensor_tensor(up[:, i * S : (i + 1) * S], wide[2 + i][:].indirect(l4[:]), hn[2 + i][:], ALU.subtract)
            for c, (j0, w) in enumerate(CHUNKS):
                nc.scalar.activation(
                    half[c][:, i * w : (i + 1) * w], up[:, i * S + j0 : i * S + j0 + w], ACT.Relu, scale=-0.5
                )
            if i == 0:
                nc.vector.scalar_tensor_tensor(
                    o_lo[:, S : 2 * S], wide[3][:, S : 2 * S], 0.0, half_lo[:], ALU.max, ALU.add
                )
                nc.sync.dma_start(out_rows[:, 0:2, :], o_lo[:].rearrange("p (t j) -> p t j", t=2))
        for c, (j0, w) in enumerate(CHUNKS):
            nc.scalar.copy(
                ob[c][:].rearrange("p (j t) -> p j t", t=PACK)[:, :, 0:2],
                o_lo[:].rearrange("p (t j) -> p j t", t=2)[:, j0 : j0 + w, :],
            )
        for c, (j0, w) in enumerate(CHUNKS):
            for i in range(2):
                nc.vector.tensor_tensor(
                    down[:, i * w0 : i * w0 + w],
                    hn[2 + i][:].indirect(entries(l3, j0, w)),
                    wide[2 + i][:, j0 : j0 + w],
                    ALU.subtract,
                )
            o_hi = sb(f"o_hi{c}", [P, 2 * w], F32)
            for i in range(2):
                cols = slice(i * w, (i + 1) * w)
                nc.vector.scalar_tensor_tensor(
                    o_hi[:, cols], down[:, i * w0 : i * w0 + w], 0.0, half[c][:, cols], ALU.max, ALU.add
                )
            nc.sync.dma_start(out_rows[:, 2:4, j0 : j0 + w], o_hi[:].rearrange("p (t j) -> p t j", t=2))
            if c == last:
                ow = sb("ow", [P, S], U32, tag="half1")
            oin = o_hi[:].rearrange("p (t j) -> p j t", t=2)
            oout = ob[c][:].rearrange("p (j t) -> p j t", t=PACK)[:, :, 2:4]
            if c == last:
                nc.vector.tensor_copy(oout, oin)
            else:
                nc.scalar.copy(oout, oin)
        for c, (j0, w) in enumerate(CHUNKS):
            nc.vector.quantize_mx(out=ow[:, j0 : j0 + w].bitcast(FP8X4), scales=osc[:, j0 : j0 + w], in_=ob[c][:])
            nc.sync.dma_start(out_words[:, j0 : j0 + w], ow[:, j0 : j0 + w].bitcast(I32))
        o_rows = out_2[0].rearrange("(q r) c -> r q c", r=4)
        for r in range(4):
            eng = nc.scalar if r % 2 else nc.sync
            eng.dma_start(o_rows[r].bitcast(I32), osc[r:P:32, :].bitcast(I32))
